import numpy as np
import ml_dtypes


def mxq(x, axis, fmt="e4m3"):
    dtype, down = {"e4m3": (ml_dtypes.float8_e4m3fn, 7), "e5m2": (ml_dtypes.float8_e5m2, 14)}[fmt]
    v = np.moveaxis(np.asarray(x, np.float32).astype(ml_dtypes.bfloat16).astype(np.float64), axis, -1)
    blocks = v.reshape(v.shape[:-1] + (-1, 32))
    amax = np.abs(blocks).max(-1, keepdims=True)
    byte = np.maximum(np.where(amax > 0, np.frexp(amax)[1] - 1 + 127, 0) - down, 1)
    scale = np.exp2(byte - 127.0)
    codes = (blocks / scale).astype(np.float32).astype(dtype).astype(np.float64)
    return np.moveaxis((codes * scale).reshape(v.shape), -1, axis)


WIDE = False


def mx_kscale(k):
    if not WIDE:
        return np.ones(k)
    levels = np.array([10, -10, 5, -5, 0])
    if k % 512:
        return np.exp2(np.random.permutation(np.resize(levels, k // 32))).repeat(32)
    a = np.empty((k // 512, 16))
    for p in range(k // 512):
        a[p, :8] = np.random.permutation(np.resize(levels, 8))
        for g in range(8):
            far = levels[np.abs(levels - a[p, g]) >= 10]
            a[p, g + 8] = far[np.random.randint(len(far))]
    return np.exp2(a.ravel()).repeat(32)


BF16 = ml_dtypes.bfloat16


def bf(x):
    return np.asarray(x, np.float32).astype(BF16)


def f64(x):
    return np.asarray(x).astype(np.float64)


E2M1 = np.array([0.0, 0.5, 1.0, 1.5, 2.0, 3.0, 4.0, 6.0, -0.0, -0.5, -1.0, -1.5, -2.0, -3.0, -4.0, -6.0])


def pack_weight(w, fmt):
    k, n = w.shape
    w = f64(bf(w)).reshape(k // 32, 32, n)
    amax = np.abs(w).max(1)
    if fmt == "e4m3":
        byte = np.frexp(amax)[1] - 1 + 127 - 7
    else:
        mant, ex = np.frexp(amax / 6.0)
        byte = np.where(mant > 0.5, ex, ex - 1) + 127
    byte = np.clip(np.where(amax > 0, byte, 1), 1, 254)
    scaled = (w * np.exp2(127.0 - byte)[:, None, :]).reshape(k, n).astype(np.float32)
    by_word = np.ascontiguousarray(scaled.reshape(k // 512, 128, 4, n).transpose(0, 1, 3, 2))
    if fmt == "e4m3":
        words = by_word.astype(ml_dtypes.float8_e4m3fn).view(np.uint8)
    else:
        c = by_word.astype(ml_dtypes.float4_e2m1fn).view(np.uint8) & 0xF
        words = c[..., 0::2] | (c[..., 1::2] << 4)
    return np.ascontiguousarray(words), np.ascontiguousarray(byte.astype(np.uint8).reshape(k // 512, 16, n))


def unpack_weight(words, scales, fmt):
    g, p, n, _ = words.shape
    if fmt == "e4m3":
        vals = np.ascontiguousarray(words).view(ml_dtypes.float8_e4m3fn).astype(np.float64)
    else:
        nib = np.empty((g, p, n, 4), np.uint8)
        nib[..., 0::2] = words & 0xF
        nib[..., 1::2] = words >> 4
        vals = E2M1[nib]
    vals = vals * np.repeat(np.exp2(scales.astype(np.float64) - 127.0), 8, axis=1)[..., None]
    return vals.transpose(0, 1, 3, 2).reshape(g * 512, n)
def pack4(w):
    words, scales = pack_weight(w, "e2m1")
    return words.reshape(words.shape[0], 128, -1), scales


def unpack4(words, scales):
    return unpack_weight(words.reshape(words.shape[0], 128, -1, 2), scales, "e2m1")


def planes(Y):
    n, m = Y.shape
    b = f64(bf(Y)).reshape(n // 32, 32, m)
    amax = np.abs(b).max(1)
    byte = np.clip(np.where(amax > 0, np.frexp(amax)[1] - 1 + 127 - 7, 1), 1, 254)
    codes = (b * np.exp2(127.0 - byte)[:, None, :]).reshape(n, m).astype(np.float32).astype(ml_dtypes.float8_e4m3fn).view(np.uint8)
    words = codes.reshape(n // 512, 128, 4, m).transpose(0, 1, 3, 2)
    return np.ascontiguousarray(words), np.ascontiguousarray(byte.astype(np.uint8).reshape(n // 512, 16, m))


M, K, L, P = 2048, 1536, 1024, 512


def setup_inputs():
    s = mx_kscale(K)
    t = mx_kscale(M)
    x = np.random.randn(M, K) / s[None, :]
    signs = np.where(np.random.randn(K) < 0, -1.0, 1.0)
    omega = np.random.randn(K, L) / np.sqrt(K) * s[:, None]
    psi = np.random.randn(M, P) / np.sqrt(M) / t[:, None]
    row_scale = np.exp(0.3 * np.random.randn(M)) * t
    running_core = 0.5 * np.random.randn(P, L)
    coef = np.exp(0.8 * np.random.randn(L))
    omega_words, omega_scales = pack4(omega)
    psi_words, psi_scales = pack4(psi)
    return {"x": bf(x), "signs": bf(signs),
            "omega_words": omega_words, "omega_scales": omega_scales,
            "row_scale": bf(row_scale),
            "psi_words": psi_words, "psi_scales": psi_scales,
            "running_core": bf(running_core), "coef": bf(coef)}

def reference(x, signs, omega_words, omega_scales, row_scale, psi_words, psi_scales, running_core, coef):
    omega = unpack4(omega_words, omega_scales)
    psi = unpack4(psi_words, psi_scales)
    a = mxq(f64(x) * f64(signs)[None, :], 1, "e4m3")
    h = (a @ omega) * f64(row_scale)[:, None]
    core = psi.T @ mxq(h, 0, "e4m3")
    y = (core + f64(running_core)) * f64(coef)[None, :]
    Y = y.T
    words, scales = planes(Y)
    return y, words, scales

@@ -1,0 +1,313 @@
+from contextlib import ExitStack
+
+import concourse.mybir as mybir
+from concourse.masks import make_identity
+
+M, K, L, PW = 2048, 1536, 1024, 512
+FLOPS = 2 * M * K * L + 2 * PW * M * L
+
+F32 = mybir.dt.float32
+BF16 = mybir.dt.bfloat16
+U32 = mybir.dt.uint32
+I32 = mybir.dt.int32
+U8 = mybir.dt.uint8
+FP8X4 = mybir.dt.float8_e4m3fn_x4
+FP4X4 = mybir.dt.float4_e2m1fn_x4
+COPY = mybir.ActivationFunctionType.Copy
+MULT = mybir.AluOpType.mult
+ADD = mybir.AluOpType.add
+
+P = 128
+KG = K // 512
+MG = M // 512
+LH = L // 512
+PAIRS = 2 * MG
+PB = PW // P
+FIRST_PERMUTED = 3
+RC_FIRST = 4
+
+
+def tile_sign_flipped_core_sketch_h1_kernel(
+    tc, x, signs, omega_words, omega_scales, row_scale, psi_words, psi_scales, running_core, coef,
+    out_0, out_1, out_2,
+):
+    nc = tc.nc
+    with ExitStack() as ctx:
+        sb = ctx.enter_context(tc.tile_pool(name="sb", bufs=1))
+        ps = ctx.enter_context(tc.psum_pool(name="ps", bufs=1))
+
+        def tiles(name, count, shape, dtype):
+            return [sb.tile(shape, dtype, name="%s%d" % (name, i), align_bytes=64) for i in range(count)]
+
+        bank = [ps.tile([P, 512], F32, name="bank%d" % i) for i in range(8)]
+        ident = sb.tile([P, P], F32, name="ident", align_bytes=64)
+        sgn = sb.tile([P, KG, 4], BF16, name="sgn", align_bytes=64)
+        rs16 = sb.tile([P, MG, 4], BF16, name="rs16", align_bytes=64)
+        rs32 = sb.tile([P, MG * 4], F32, name="rs32", align_bytes=64)
+        cf16 = sb.tile([P, LH, 4], BF16, name="cf16", align_bytes=64)
+        cf32 = sb.tile([P, LH * 4], F32, name="cf32", align_bytes=64)
+        om = tiles("om", LH, [P, KG, 1024], U8)
+        om_sc = sb.tile([P, KG, L], U8, name="om_sc", align_bytes=64)
+        psi = sb.tile([P, MG, 2 * PW], U8, name="psi", align_bytes=64)
+        psi_sc = sb.tile([P, MG, PW], U8, name="psi_sc", align_bytes=64)
+        x0 = tiles("x0_", KG, [P, 2, 512], BF16)
+        xs = [None] + tiles("xs", PAIRS - 1, [P, 2, K], BF16)
+        xp = tiles("xp", 2, [P, 2 * KG, 2, P], F32)
+        a16 = tiles("a16_", 3, [P, 1024], BF16)
+        a_cd = [tiles("a_cd%d_" % i, KG, [P, 256], U32) for i in range(2)]
+        a_sc = [tiles("a_sc%d_" % i, KG, [P, 256], U8) for i in range(2)]
+        h16 = tiles("h16_", 4, [P, 4, 512], BF16)
+        hin = tiles("hin", 2, [P, 2048], BF16)
+        h_cd = tiles("h_cd", MG * LH, [P, 512], U32)
+        h_sc = tiles("h_sc", MG * LH, [P, 512], U8)
+        rc = sb.tile([P, PB, L], BF16, name="rc", align_bytes=64)
+        rcc = tiles("rcc", LH * 4, [P, PW], F32)
+        yf = [sb.tile([P, 4, PW], F32, name="yfull%d" % h, align_bytes=64) for h in range(LH)]
+        y16 = tiles("y16_", LH, [P, 2048], BF16)
+        y_cd = tiles("y_cd", LH, [P, PW], U32)
+        y_sc = tiles("y_sc", LH, [P, PW], U8)
+        yo = tiles("yo", LH * PB, [P, 512], F32)
+
+        ctx.enter_context(tc.manual_schedule())
+
+        def x_rows(j):
+            rows = x[512 * (j // 2): 512 * (j // 2 + 1), :].rearrange("(c t) k -> c t k", t=4)
+            return rows[:, 2 * (j % 2): 2 * (j % 2) + 2, :]
+
+        def load_scales(plane, scales):
+            for q in range(4):
+                nc.sync.dma_start(
+                    out=plane[32 * q: 32 * q + 4, :, :].bitcast(I32),
+                    in_=scales[:, 4 * q: 4 * q + 4, :].rearrange("g r n -> r g n").bitcast(I32),
+                )
+
+        def load_om(h):
+            nc.sync.dma_start(
+                out=om[h][:].bitcast(I32),
+                in_=omega_words[:, :, 1024 * h: 1024 * (h + 1)].rearrange("g p b -> p g b").bitcast(I32),
+            )
+
+        make_identity(nc, ident[:])
+        nc.vector.memset(om_sc[:].rearrange("p g n -> p (g n)").bitcast(I32), 0)
+        nc.vector.memset(psi_sc[:].rearrange("p g n -> p (g n)").bitcast(I32), 0)
+        nc.scalar.dma_start(out=sgn[:], in_=signs.rearrange("(g c t) -> c g t", c=P, t=4))
+        nc.scalar.dma_start(out=rs16[:], in_=row_scale.rearrange("(g c t) -> c g t", c=P, t=4))
+        nc.sync.dma_start(out=x0[0][:], in_=x_rows(0)[:, :, 0:512])
+        nc.sync.dma_start(out=x0[1][:], in_=x_rows(0)[:, :, 512:1024])
+        load_scales(om_sc, omega_scales)
+        nc.sync.dma_start(out=x0[2][:], in_=x_rows(0)[:, :, 1024:1536])
+        load_om(0)
+        nc.sync.dma_start(out=xs[1][:], in_=x_rows(1))
+        load_om(1)
+        for j in range(2, 5):
+            nc.sync.dma_start(out=xs[j][:], in_=x_rows(j))
+        nc.sync.dma_start(out=cf16[:], in_=coef.rearrange("(h c t) -> c h t", c=P, t=4))
+        nc.sync.dma_start(out=rc[:], in_=running_core.rearrange("(b p) l -> p b l", p=P))
+        for j in range(5, PAIRS):
+            nc.sync.dma_start(out=xs[j][:], in_=x_rows(j))
+        load_scales(psi_sc, psi_scales)
+        nc.sync.dma_start(out=psi[:].bitcast(I32), in_=psi_words.rearrange("g p b -> p g b").bitcast(I32))
+        nc.scalar.activation(out=rs32[:], in_=rs16[:].rearrange("p g t -> p (g t)"), func=COPY)
+
+        def permute(j):
+            words = xs[j][:].rearrange("p s k -> p (s k)").bitcast(F32)
+            nc.scalar.copy(out=xp[j % 2][:], in_=words.rearrange("p (a c u) -> p a u c", c=P, u=2))
+
+        def turn_x(j, g):
+            for u in range(2):
+                for s in range(2):
+                    if j == 0:
+                        src = x0[g][:, s, :].bitcast(F32)[:, u:256:2]
+                    elif j < FIRST_PERMUTED:
+                        src = xs[j][:, s, :].bitcast(F32)[:, 256 * g + u: 256 * (g + 1): 2]
+                    else:
+                        src = xp[j % 2][:, KG * s + g, u, :]
+                    slot = 2 * u + s
+                    nc.tensor.transpose(bank[4 + g][:, P * slot: P * (slot + 1)], src, ident[:])
+
+        def sign_out(g):
+            nc.vector.tensor_tensor(
+                out=a16[g][:].rearrange("p (r u e) -> p r u e", u=2, e=2),
+                in0=bank[4 + g][:].bitcast(BF16).rearrange("p (u r e) -> p r u e", u=2, e=2),
+                in1=sgn[:, g, :].rearrange("p (u e) -> p u e", u=2).unsqueeze(1).to_broadcast([P, 256, 2, 2]),
+                op=MULT,
+            )
+
+        def quant_a(j, g):
+            nc.vector.quantize_mx(out=a_cd[j % 2][g][:].bitcast(FP8X4), scales=a_sc[j % 2][g][:], in_=a16[g][:])
+
+        def mm1(j, h, s, g):
+            nc.tensor.matmul_mx(
+                out=bank[2 * h + s][:],
+                lhsT=a_cd[j % 2][g][:, P * s: P * (s + 1)].bitcast(FP8X4),
+                lhsT_scale=a_sc[j % 2][g][:, P * s: P * (s + 1)],
+                rhs=om[h][:, g, :].bitcast(FP4X4),
+                rhs_scale=om_sc[:, g, 512 * h: 512 * (h + 1)],
+                start=(g == 0),
+                stop=(g == KG - 1),
+            )
+
+        def evac_h(j, h, s):
+            grp, t = j // 2, 2 * (j % 2) + s
+            nc.scalar.activation(
+                out=h16[(2 * grp + h) % 4][:, t, :].rearrange("p (a c) -> p a c", a=4),
+                in_=bank[2 * h + s][:].rearrange("p (c a) -> p a c", a=4),
+                func=COPY,
+                scale=rs32[:, 4 * grp + t: 4 * grp + t + 1],
+            )
+
+        def tile1(j, h, s):
+            for g in range(KG):
+                mm1(j, h, s, g)
+            evac_h(j, h, s)
+
+        def weave_h(n):
+            nc.vector.tensor_copy(
+                out=hin[n % 2][:].rearrange("p (n t) -> p n t", t=4),
+                in_=h16[n % 4][:].rearrange("p t n -> p n t"),
+            )
+
+        def quant_h(n):
+            nc.vector.quantize_mx(out=h_cd[n][:].bitcast(FP8X4), scales=h_sc[n][:], in_=hin[n % 2][:])
+
+        def turn_rc(h, u):
+            for b in range(PB):
+                src = rc[:, b, :].bitcast(F32)[:, 256 * h + u: 256 * (h + 1): 2]
+                nc.tensor.transpose(bank[7][:, P * b: P * (b + 1)], src, ident[:])
+
+        def scale_rc(h, u, e):
+            i = 4 * h + 2 * u + e
+            nc.scalar.activation(
+                out=rcc[i][:],
+                in_=bank[7][:].bitcast(BF16).rearrange("p (n e) -> p e n", e=2)[:, e, :],
+                func=COPY,
+                scale=cf32[:, i: i + 1],
+            )
+
+        def bank2(h, a):
+            return bank[4 * (1 - h) + a]
+
+        def mm2(h, a, grp):
+            n = 2 * grp + h
+            nc.tensor.matmul_mx(
+                out=bank2(h, a)[:],
+                lhsT=h_cd[n][:, P * a: P * (a + 1)].bitcast(FP8X4),
+                lhsT_scale=h_sc[n][:, P * a: P * (a + 1)],
+                rhs=psi[:, grp, :].bitcast(FP4X4),
+                rhs_scale=psi_sc[:, grp, :],
+                start=(grp == 0),
+                stop=(grp == MG - 1),
+            )
+
+        def finish_y(h, a):
+            i = 4 * h + a
+            nc.vector.scalar_tensor_tensor(
+                out=yf[h][:, a, :], in0=bank2(h, a)[:], scalar=cf32[:, i: i + 1], in1=rcc[i][:], op0=MULT, op1=ADD
+            )
+
+        def weave_y(h):
+            nc.vector.tensor_copy(
+                out=y16[h][:].rearrange("p (n t) -> p n t", t=4), in_=yf[h][:].rearrange("p t n -> p n t")
+            )
+
+        def quant_y(h):
+            nc.vector.quantize_mx(out=y_cd[h][:].bitcast(FP8X4), scales=y_sc[h][:], in_=y16[h][:])
+
+        def store_planes(h):
+            nc.sync.dma_start(out=out_1[h].rearrange("p m t -> p (m t)").bitcast(I32), in_=y_cd[h][:].bitcast(I32))
+            for q in range(4):
+                nc.sync.dma_start(
+                    out=out_2[h, 4 * q: 4 * q + 4, :].bitcast(I32), in_=y_sc[h][32 * q: 32 * q + 4, :].bitcast(I32)
+                )
+
+        def turn_y(h, a, b):
+            nc.tensor.transpose(bank[4 + b][:, P * a: P * (a + 1)], yf[h][:, a, P * b: P * (b + 1)], ident[:])
+
+        def out_y(h, b):
+            nc.scalar.copy(
+                out=yo[PB * h + b][:].rearrange("p (c a) -> p c a", a=4),
+                in_=bank[4 + b][:].rearrange("p (a c) -> p c a", a=4),
+            )
+            nc.sync.dma_start(out=out_0[P * b: P * (b + 1), 512 * h: 512 * (h + 1)], in_=yo[PB * h + b][:])
+
+        def turn_step(j, n):
+            for g in range(KG):
+                turn_x(j, g)
+            r = j - RC_FIRST
+            if 0 <= r < 4:
+                turn_rc(r // 2, r % 2)
+            sign_out(0)
+            sign_out(1)
+            quant_a(j, 0)
+            sign_out(2)
+            quant_a(j, 1)
+            if n is not None:
+                weave_h(n)
+            quant_a(j, 2)
+            if n is not None:
+                quant_h(n)
+
+        turn_step(0, None)
+        for g in range(KG):
+            for s in range(2):
+                mm1(0, 0, s, g)
+        for s in range(2):
+            evac_h(0, 0, s)
+        turn_step(1, None)
+        for s in range(2):
+            tile1(0, 1, s)
+
+        for j in range(1, PAIRS):
+            n = j - 2 if j >= 2 else None
+            if j + 1 < PAIRS:
+                turn_step(j + 1, n)
+            else:
+                weave_h(n)
+                quant_h(n)
+            if j == 1:
+                nc.scalar.activation(out=cf32[:], in_=cf16[:].rearrange("p h t -> p (h t)"), func=COPY)
+            if FIRST_PERMUTED <= j + 2 < PAIRS:
+                permute(j + 2)
+            r = j + 1 - RC_FIRST
+            for h in range(LH):
+                for s in range(2):
+                    tile1(j, h, s)
+                if 0 <= r < 4:
+                    scale_rc(r // 2, r % 2, h)
+
+        weave_h(6)
+        quant_h(6)
+        weave_h(7)
+        quant_h(7)
+        for a in range(2):
+            for grp in range(MG - 1):
+                mm2(0, a, grp)
+        for a in range(2):
+            mm2(0, a, MG - 1)
+            finish_y(0, a)
+        for a in range(2, 4):
+            for grp in range(MG):
+                mm2(0, a, grp)
+            finish_y(0, a)
+        for a in range(4):
+            for grp in range(MG):
+                mm2(1, a, grp)
+            if a == 0:
+                weave_y(0)
+            finish_y(1, a)
+            if a == 0:
+                quant_y(0)
+                store_planes(0)
+                for b in range(PB):
+                    for t in range(4):
+                        turn_y(0, t, b)
+                    out_y(0, b)
+        for t in range(3):
+            for b in range(PB):
+                turn_y(1, t, b)
+        weave_y(1)
+        for b in range(PB):
+            turn_y(1, 3, b)
+            out_y(1, b)
+        quant_y(1)
+        store_planes(1)

@@ -23,8 +23,10 @@ MG = M // 512
 LH = L // 512
 PAIRS = 2 * MG
 PB = PW // P
-FIRST_PERMUTED = 3
-RC_FIRST = 4
+CHUNKED = 3
+DIRECT = ()
+B2 = ((4, 5, 0, 1), (2, 3, 6, 7))
+BT = (4, 5, 0, 1)
 
 
 def tile_sign_flipped_core_sketch_h1_kernel(
@@ -47,12 +49,13 @@ def tile_sign_flipped_core_sketch_h1_kernel(
         cf16 = sb.tile([P, LH, 4], BF16, name="cf16", align_bytes=64)
         cf32 = sb.tile([P, LH * 4], F32, name="cf32", align_bytes=64)
         om = tiles("om", LH, [P, KG, 1024], U8)
-        om_sc = sb.tile([P, KG, L], U8, name="om_sc", align_bytes=64)
+        om_sc = tiles("om_sc", LH, [P, KG, 512], U8)
         psi = sb.tile([P, MG, 2 * PW], U8, name="psi", align_bytes=64)
         psi_sc = sb.tile([P, MG, PW], U8, name="psi_sc", align_bytes=64)
-        x0 = tiles("x0_", KG, [P, 2, 512], BF16)
-        xs = [None] + tiles("xs", PAIRS - 1, [P, 2, K], BF16)
-        xp = tiles("xp", 2, [P, 2 * KG, 2, P], F32)
+        xc = [tiles("xc%d_" % j, KG, [P, 2, 512], BF16) for j in range(CHUNKED)]
+        xw = tiles("xw", PAIRS - CHUNKED, [P, 2, K], BF16)
+        xp = [tiles("xp%d_" % i, KG, [P, 2, 2, P], F32) for i in range(2)]
+        rcp = tiles("rcp", LH, [P, PB, 2, P], F32)
         a16 = tiles("a16_", 3, [P, 1024], BF16)
         a_cd = [tiles("a_cd%d_" % i, KG, [P, 256], U32) for i in range(2)]
         a_sc = [tiles("a_sc%d_" % i, KG, [P, 256], U8) for i in range(2)]
@@ -66,13 +69,18 @@ def tile_sign_flipped_core_sketch_h1_kernel(
         y16 = tiles("y16_", LH, [P, 2048], BF16)
         y_cd = tiles("y_cd", LH, [P, PW], U32)
         y_sc = tiles("y_sc", LH, [P, PW], U8)
-        yo = tiles("yo", LH * PB, [P, 512], F32)
+        yo = tiles("yo", 6, [P, 512], F32)
 
         ctx.enter_context(tc.manual_schedule())
 
         def x_rows(j):
             rows = x[512 * (j // 2): 512 * (j // 2 + 1), :].rearrange("(c t) k -> c t k", t=4)
             return rows[:, 2 * (j % 2): 2 * (j % 2) + 2, :]
+
+        def x_chunk(j, g):
+            if j < CHUNKED:
+                return xc[j][g][:]
+            return xw[j - CHUNKED][:, :, 512 * g: 512 * (g + 1)]
 
         def load_scales(plane, scales):
             for q in range(4):
@@ -81,47 +89,55 @@ def tile_sign_flipped_core_sketch_h1_kernel(
                     in_=scales[:, 4 * q: 4 * q + 4, :].rearrange("g r n -> r g n").bitcast(I32),
                 )
 
-        def load_om(h):
+        def load_om(h, g0, g1):
             nc.sync.dma_start(
-                out=om[h][:].bitcast(I32),
-                in_=omega_words[:, :, 1024 * h: 1024 * (h + 1)].rearrange("g p b -> p g b").bitcast(I32),
+                out=om[h][:, g0:g1, :].bitcast(I32),
+                in_=omega_words[g0:g1, :, 1024 * h: 1024 * (h + 1)].rearrange("g p b -> p g b").bitcast(I32),
             )
 
+        def load_x(j, g):
+            nc.sync.dma_start(out=x_chunk(j, g), in_=x_rows(j)[:, :, 512 * g: 512 * (g + 1)])
+
         make_identity(nc, ident[:])
-        nc.vector.memset(om_sc[:].rearrange("p g n -> p (g n)").bitcast(I32), 0)
+        nc.vector.memset(om_sc[0][:].rearrange("p g n -> p (g n)").bitcast(I32), 0)
+        nc.vector.memset(om_sc[1][:].rearrange("p g n -> p (g n)").bitcast(I32), 0)
         nc.vector.memset(psi_sc[:].rearrange("p g n -> p (g n)").bitcast(I32), 0)
         nc.scalar.dma_start(out=sgn[:], in_=signs.rearrange("(g c t) -> c g t", c=P, t=4))
-        nc.scalar.dma_start(out=rs16[:], in_=row_scale.rearrange("(g c t) -> c g t", c=P, t=4))
-        nc.sync.dma_start(out=x0[0][:], in_=x_rows(0)[:, :, 0:512])
-        nc.sync.dma_start(out=x0[1][:], in_=x_rows(0)[:, :, 512:1024])
-        load_scales(om_sc, omega_scales)
-        nc.sync.dma_start(out=x0[2][:], in_=x_rows(0)[:, :, 1024:1536])
-        load_om(0)
-        nc.sync.dma_start(out=xs[1][:], in_=x_rows(1))
-        load_om(1)
-        for j in range(2, 5):
-            nc.sync.dma_start(out=xs[j][:], in_=x_rows(j))
+        load_x(0, 0)
+        load_scales(om_sc[0], omega_scales[:, :, 0:512])
+        load_x(0, 1)
+        load_x(0, 2)
+        load_om(0, 0, KG)
+        nc.sync.dma_start(out=rs16[:], in_=row_scale.rearrange("(g c t) -> c g t", c=P, t=4))
+        for g in range(KG):
+            load_x(1, g)
+        load_scales(om_sc[1], omega_scales[:, :, 512:1024])
+        load_om(1, 0, KG)
+        for j in range(2, PAIRS):
+            if j < CHUNKED:
+                for g in range(KG):
+                    load_x(j, g)
+            else:
+                nc.sync.dma_start(out=xw[j - CHUNKED][:], in_=x_rows(j))
         nc.sync.dma_start(out=cf16[:], in_=coef.rearrange("(h c t) -> c h t", c=P, t=4))
         nc.sync.dma_start(out=rc[:], in_=running_core.rearrange("(b p) l -> p b l", p=P))
-        for j in range(5, PAIRS):
-            nc.sync.dma_start(out=xs[j][:], in_=x_rows(j))
         load_scales(psi_sc, psi_scales)
         nc.sync.dma_start(out=psi[:].bitcast(I32), in_=psi_words.rearrange("g p b -> p g b").bitcast(I32))
-        nc.scalar.activation(out=rs32[:], in_=rs16[:].rearrange("p g t -> p (g t)"), func=COPY)
 
-        def permute(j):
-            words = xs[j][:].rearrange("p s k -> p (s k)").bitcast(F32)
-            nc.scalar.copy(out=xp[j % 2][:], in_=words.rearrange("p (a c u) -> p a u c", c=P, u=2))
+
+        def permute(j, g, copy):
+            if j in DIRECT:
+                return
+            words = x_chunk(j, g).bitcast(F32)
+            copy(out=xp[j % 2][g][:], in_=words.rearrange("p s (c u) -> p s u c", u=2))
 
         def turn_x(j, g):
             for u in range(2):
                 for s in range(2):
-                    if j == 0:
-                        src = x0[g][:, s, :].bitcast(F32)[:, u:256:2]
-                    elif j < FIRST_PERMUTED:
-                        src = xs[j][:, s, :].bitcast(F32)[:, 256 * g + u: 256 * (g + 1): 2]
+                    if j in DIRECT:
+                        src = x_chunk(j, g)[:, s, :].bitcast(F32)[:, u:256:2]
                     else:
-                        src = xp[j % 2][:, KG * s + g, u, :]
+                        src = xp[j % 2][g][:, s, u, :]
                     slot = 2 * u + s
                     nc.tensor.transpose(bank[4 + g][:, P * slot: P * (slot + 1)], src, ident[:])
 
@@ -142,7 +158,7 @@ def tile_sign_flipped_core_sketch_h1_kernel(
                 lhsT=a_cd[j % 2][g][:, P * s: P * (s + 1)].bitcast(FP8X4),
                 lhsT_scale=a_sc[j % 2][g][:, P * s: P * (s + 1)],
                 rhs=om[h][:, g, :].bitcast(FP4X4),
-                rhs_scale=om_sc[:, g, 512 * h: 512 * (h + 1)],
+                rhs_scale=om_sc[h][:, g, :],
                 start=(g == 0),
                 stop=(g == KG - 1),
             )
@@ -161,31 +177,33 @@ def tile_sign_flipped_core_sketch_h1_kernel(
                 mm1(j, h, s, g)
             evac_h(j, h, s)
 
-        def weave_h(n):
-            nc.vector.tensor_copy(
-                out=hin[n % 2][:].rearrange("p (n t) -> p n t", t=4),
-                in_=h16[n % 4][:].rearrange("p t n -> p n t"),
+        def weave_h(n, copy):
+            copy(
+                out=hin[n % 2][:].rearrange("p (c i t) -> p c t i", i=4, t=4),
+                in_=h16[n % 4][:].rearrange("p t (c i) -> p c t i", i=4),
             )
 
         def quant_h(n):
             nc.vector.quantize_mx(out=h_cd[n][:].bitcast(FP8X4), scales=h_sc[n][:], in_=hin[n % 2][:])
 
+        def permute_rc(h):
+            words = rc[:, :, 512 * h: 512 * (h + 1)].bitcast(F32)
+            nc.scalar.copy(out=rcp[h][:], in_=words.rearrange("p b (c u) -> p b u c", u=2))
+
         def turn_rc(h, u):
             for b in range(PB):
-                src = rc[:, b, :].bitcast(F32)[:, 256 * h + u: 256 * (h + 1): 2]
-                nc.tensor.transpose(bank[7][:, P * b: P * (b + 1)], src, ident[:])
+                nc.tensor.transpose(bank[4 + 2 * h + u][:, P * b: P * (b + 1)], rcp[h][:, b, u, :], ident[:])
 
         def scale_rc(h, u, e):
             i = 4 * h + 2 * u + e
-            nc.scalar.activation(
-                out=rcc[i][:],
-                in_=bank[7][:].bitcast(BF16).rearrange("p (n e) -> p e n", e=2)[:, e, :],
-                func=COPY,
-                scale=cf32[:, i: i + 1],
-            )
+            src = bank[4 + 2 * h + u][:].bitcast(BF16).rearrange("p (n e) -> p e n", e=2)[:, e, :]
+            if h == 0:
+                nc.vector.tensor_scalar(out=rcc[i][:], in0=src, scalar1=cf32[:, i: i + 1], scalar2=None, op0=MULT)
+            else:
+                nc.scalar.activation(out=rcc[i][:], in_=src, func=COPY, scale=cf32[:, i: i + 1])
 
         def bank2(h, a):
-            return bank[4 * (1 - h) + a]
+            return bank[B2[h][a]]
 
         def mm2(h, a, grp):
             n = 2 * grp + h
@@ -199,92 +217,123 @@ def tile_sign_flipped_core_sketch_h1_kernel(
                 stop=(grp == MG - 1),
             )
 
-        def finish_y(h, a):
+        def finish_y(h, a, c0=0, c1=PW):
             i = 4 * h + a
             nc.vector.scalar_tensor_tensor(
-                out=yf[h][:, a, :], in0=bank2(h, a)[:], scalar=cf32[:, i: i + 1], in1=rcc[i][:], op0=MULT, op1=ADD
+                out=yf[h][:, a, c0:c1], in0=bank2(h, a)[:, c0:c1], scalar=cf32[:, i: i + 1], in1=rcc[i][:, c0:c1],
+                op0=MULT, op1=ADD,
             )
 
-        def weave_y(h):
+        def weave_y(h, c0=0, c1=PW):
             nc.vector.tensor_copy(
-                out=y16[h][:].rearrange("p (n t) -> p n t", t=4), in_=yf[h][:].rearrange("p t n -> p n t")
+                out=y16[h][:, 4 * c0: 4 * c1].rearrange("p (c i t) -> p c t i", i=4, t=4),
+                in_=yf[h][:, :, c0:c1].rearrange("p t (c i) -> p c t i", i=4),
             )
 
-        def quant_y(h):
-            nc.vector.quantize_mx(out=y_cd[h][:].bitcast(FP8X4), scales=y_sc[h][:], in_=y16[h][:])
+        def quant_y(h, c0=0, c1=PW):
+            nc.vector.quantize_mx(
+                out=y_cd[h][:, c0:c1].bitcast(FP8X4), scales=y_sc[h][:, c0:c1], in_=y16[h][:, 4 * c0: 4 * c1]
+            )
 
-        def store_planes(h):
-            nc.sync.dma_start(out=out_1[h].rearrange("p m t -> p (m t)").bitcast(I32), in_=y_cd[h][:].bitcast(I32))
+        def store_words(h, c0=0, c1=PW):
+            nc.sync.dma_start(
+                out=out_1[h, :, c0:c1, :].rearrange("p m t -> p (m t)").bitcast(I32), in_=y_cd[h][:, c0:c1].bitcast(I32)
+            )
+
+        def store_scales(h):
             for q in range(4):
                 nc.sync.dma_start(
                     out=out_2[h, 4 * q: 4 * q + 4, :].bitcast(I32), in_=y_sc[h][32 * q: 32 * q + 4, :].bitcast(I32)
                 )
 
         def turn_y(h, a, b):
-            nc.tensor.transpose(bank[4 + b][:, P * a: P * (a + 1)], yf[h][:, a, P * b: P * (b + 1)], ident[:])
+            nc.tensor.transpose(bank[BT[b]][:, P * a: P * (a + 1)], yf[h][:, a, P * b: P * (b + 1)], ident[:])
 
         def out_y(h, b):
+            dst = yo[(PB * h + b) % 6]
             nc.scalar.copy(
-                out=yo[PB * h + b][:].rearrange("p (c a) -> p c a", a=4),
-                in_=bank[4 + b][:].rearrange("p (a c) -> p c a", a=4),
+                out=dst[:].rearrange("p (c a) -> p c a", a=4),
+                in_=bank[BT[b]][:].rearrange("p (a c) -> p c a", a=4),
             )
-            nc.sync.dma_start(out=out_0[P * b: P * (b + 1), 512 * h: 512 * (h + 1)], in_=yo[PB * h + b][:])
+            nc.sync.dma_start(out=out_0[P * b: P * (b + 1), 512 * h: 512 * (h + 1)], in_=dst[:])
 
-        def turn_step(j, n):
+        def turn_step(j, pending):
             for g in range(KG):
                 turn_x(j, g)
-            r = j - RC_FIRST
-            if 0 <= r < 4:
-                turn_rc(r // 2, r % 2)
             sign_out(0)
+            if pending is not None:
+                quant_h(pending)
             sign_out(1)
             quant_a(j, 0)
             sign_out(2)
             quant_a(j, 1)
-            if n is not None:
-                weave_h(n)
             quant_a(j, 2)
-            if n is not None:
-                quant_h(n)
 
-        turn_step(0, None)
+        permute(0, 0, nc.vector.tensor_copy)
+        permute(0, 1, nc.vector.tensor_copy)
+        permute(0, 2, nc.scalar.copy)
+        nc.scalar.activation(out=rs32[:], in_=rs16[:].rearrange("p g t -> p (g t)"), func=COPY)
+        for g in range(KG):
+            turn_x(0, g)
+            sign_out(g)
+            quant_a(0, g)
+        for g in range(KG):
+            permute(1, g, nc.scalar.copy)
         for g in range(KG):
             for s in range(2):
                 mm1(0, 0, s, g)
         for s in range(2):
             evac_h(0, 0, s)
         turn_step(1, None)
-        for s in range(2):
-            tile1(0, 1, s)
+        for g in range(KG):
+            permute(2, g, nc.scalar.copy)
+        tile1(0, 1, 0)
+        tile1(0, 1, 1)
 
         for j in range(1, PAIRS):
-            n = j - 2 if j >= 2 else None
             if j + 1 < PAIRS:
-                turn_step(j + 1, n)
+                turn_step(j + 1, j - 2 if j >= 2 else None)
             else:
-                weave_h(n)
-                quant_h(n)
-            if j == 1:
+                for h in range(LH):
+                    for u in range(2):
+                        turn_rc(h, u)
+                scale_rc(0, 0, 0)
+                quant_h(j - 2)
+                scale_rc(0, 0, 1)
+                scale_rc(0, 1, 0)
+                scale_rc(0, 1, 1)
+            if j % 2 == 0:
+                weave_h(j - 1, nc.vector.tensor_copy)
+            if j == 5:
                 nc.scalar.activation(out=cf32[:], in_=cf16[:].rearrange("p h t -> p (h t)"), func=COPY)
-            if FIRST_PERMUTED <= j + 2 < PAIRS:
-                permute(j + 2)
-            r = j + 1 - RC_FIRST
-            for h in range(LH):
-                for s in range(2):
-                    tile1(j, h, s)
-                if 0 <= r < 4:
-                    scale_rc(r // 2, r % 2, h)
+            side = []
+            if j + 2 < PAIRS:
+                side = [lambda g=g: permute(j + 2, g, nc.scalar.copy) for g in range(KG)]
+            elif j + 2 == PAIRS:
+                side = [lambda h=h: permute_rc(h) for h in range(LH)]
+            for work in side[:2]:
+                work()
+            tile1(j, 0, 0)
+            for work in side[2:]:
+                work()
+            tile1(j, 0, 1)
+            if j % 2 == 1:
+                weave_h(j - 1, nc.vector.tensor_copy)
+            tile1(j, 1, 0)
+            tile1(j, 1, 1)
 
-        weave_h(6)
         quant_h(6)
-        weave_h(7)
-        quant_h(7)
+        weave_h(7, nc.scalar.copy)
+        for u in range(2):
+            for e in range(2):
+                scale_rc(1, u, e)
         for a in range(2):
             for grp in range(MG - 1):
                 mm2(0, a, grp)
         for a in range(2):
             mm2(0, a, MG - 1)
             finish_y(0, a)
+        quant_h(7)
         for a in range(2, 4):
             for grp in range(MG):
                 mm2(0, a, grp)
@@ -294,20 +343,27 @@ def tile_sign_flipped_core_sketch_h1_kernel(
                 mm2(1, a, grp)
             if a == 0:
                 weave_y(0)
-            finish_y(1, a)
-            if a == 0:
-                quant_y(0)
-                store_planes(0)
                 for b in range(PB):
                     for t in range(4):
                         turn_y(0, t, b)
                     out_y(0, b)
-        for t in range(3):
-            for b in range(PB):
-                turn_y(1, t, b)
-        weave_y(1)
-        for b in range(PB):
-            turn_y(1, 3, b)
-            out_y(1, b)
-        quant_y(1)
-        store_planes(1)
+            if a < 3:
+                finish_y(1, a)
+            if a == 0:
+                quant_y(0)
+                store_words(0)
+                store_scales(0)
+        finish_y(1, 3, 0, 256)
+        finish_y(1, 3, 256, 512)
+        for half in range(2):
+            for b in (2 * half, 2 * half + 1):
+                for t in range(3):
+                    turn_y(1, t, b)
+            for b in (2 * half, 2 * half + 1):
+                turn_y(1, 3, b)
+                out_y(1, b)
+            weave_y(1, 256 * half, 256 * (half + 1))
+        for half in range(2):
+            quant_y(1, 256 * half, 256 * (half + 1))
+            store_words(1, 256 * half, 256 * (half + 1))
+        store_scales(1)

@@ -25,8 +25,8 @@ PAIRS = 2 * MG
 PB = PW // P
 CHUNKED = 3
 DIRECT = ()
-B2 = ((4, 5, 0, 1), (2, 3, 6, 7))
-BT = (4, 5, 0, 1)
+B2 = (4, 5, 6, 7, 0, 1, 2, 3)
+POOL_MUL = ()
 
 
 def tile_sign_flipped_core_sketch_h1_kernel(
@@ -46,8 +46,7 @@ def tile_sign_flipped_core_sketch_h1_kernel(
         sgn = sb.tile([P, KG, 4], BF16, name="sgn", align_bytes=64)
         rs16 = sb.tile([P, MG, 4], BF16, name="rs16", align_bytes=64)
         rs32 = sb.tile([P, MG * 4], F32, name="rs32", align_bytes=64)
-        cf16 = sb.tile([P, LH, 4], BF16, name="cf16", align_bytes=64)
-        cf32 = sb.tile([P, LH * 4], F32, name="cf32", align_bytes=64)
+        cf = sb.tile([P, L], BF16, name="cf", align_bytes=64)
         om = tiles("om", LH, [P, KG, 1024], U8)
         om_sc = tiles("om_sc", LH, [P, KG, 512], U8)
         psi = sb.tile([P, MG, 2 * PW], U8, name="psi", align_bytes=64)
@@ -55,7 +54,6 @@ def tile_sign_flipped_core_sketch_h1_kernel(
         xc = [tiles("xc%d_" % j, KG, [P, 2, 512], BF16) for j in range(CHUNKED)]
         xw = tiles("xw", PAIRS - CHUNKED, [P, 2, K], BF16)
         xp = [tiles("xp%d_" % i, KG, [P, 2, 2, P], F32) for i in range(2)]
-        rcp = tiles("rcp", LH, [P, PB, 2, P], F32)
         a16 = tiles("a16_", 3, [P, 1024], BF16)
         a_cd = [tiles("a_cd%d_" % i, KG, [P, 256], U32) for i in range(2)]
         a_sc = [tiles("a_sc%d_" % i, KG, [P, 256], U8) for i in range(2)]
@@ -64,12 +62,12 @@ def tile_sign_flipped_core_sketch_h1_kernel(
         h_cd = tiles("h_cd", MG * LH, [P, 512], U32)
         h_sc = tiles("h_sc", MG * LH, [P, 512], U8)
         rc = sb.tile([P, PB, L], BF16, name="rc", align_bytes=64)
-        rcc = tiles("rcc", LH * 4, [P, PW], F32)
-        yf = [sb.tile([P, 4, PW], F32, name="yfull%d" % h, align_bytes=64) for h in range(LH)]
+        shifted = tiles("shifted", 3, [P, 512], F32)
+        yo = tiles("yo", LH * PB, [P, 512], F32)
+        yw = tiles("yw", LH * PB, [P, 2, P, 2], BF16)
         y16 = tiles("y16_", LH, [P, 2048], BF16)
         y_cd = tiles("y_cd", LH, [P, PW], U32)
-        y_sc = tiles("y_sc", LH, [P, PW], U8)
-        yo = tiles("yo", 6, [P, 512], F32)
+        y_sc = sb.tile([P, LH, PW], U8, name="y_sc", align_bytes=64)
 
         ctx.enter_context(tc.manual_schedule())
 
@@ -103,12 +101,12 @@ def tile_sign_flipped_core_sketch_h1_kernel(
         nc.vector.memset(om_sc[1][:].rearrange("p g n -> p (g n)").bitcast(I32), 0)
         nc.vector.memset(psi_sc[:].rearrange("p g n -> p (g n)").bitcast(I32), 0)
         nc.scalar.dma_start(out=sgn[:], in_=signs.rearrange("(g c t) -> c g t", c=P, t=4))
+        nc.scalar.dma_start(out=rs16[:], in_=row_scale.rearrange("(g c t) -> c g t", c=P, t=4))
         load_x(0, 0)
         load_scales(om_sc[0], omega_scales[:, :, 0:512])
         load_x(0, 1)
         load_x(0, 2)
         load_om(0, 0, KG)
-        nc.sync.dma_start(out=rs16[:], in_=row_scale.rearrange("(g c t) -> c g t", c=P, t=4))
         for g in range(KG):
             load_x(1, g)
         load_scales(om_sc[1], omega_scales[:, :, 512:1024])
@@ -119,10 +117,10 @@ def tile_sign_flipped_core_sketch_h1_kernel(
                     load_x(j, g)
             else:
                 nc.sync.dma_start(out=xw[j - CHUNKED][:], in_=x_rows(j))
-        nc.sync.dma_start(out=cf16[:], in_=coef.rearrange("(h c t) -> c h t", c=P, t=4))
         nc.sync.dma_start(out=rc[:], in_=running_core.rearrange("(b p) l -> p b l", p=P))
         load_scales(psi_sc, psi_scales)
         nc.sync.dma_start(out=psi[:].bitcast(I32), in_=psi_words.rearrange("g p b -> p g b").bitcast(I32))
+        nc.sync.dma_start(out=cf[:], in_=coef.partition_broadcast(P))
 
 
         def permute(j, g, copy):
@@ -166,8 +164,8 @@ def tile_sign_flipped_core_sketch_h1_kernel(
         def evac_h(j, h, s):
             grp, t = j // 2, 2 * (j % 2) + s
             nc.scalar.activation(
-                out=h16[(2 * grp + h) % 4][:, t, :].rearrange("p (a c) -> p a c", a=4),
-                in_=bank[2 * h + s][:].rearrange("p (c a) -> p a c", a=4),
+                out=h16[(2 * grp + h) % 4][:, t, :],
+                in_=bank[2 * h + s][:],
                 func=COPY,
                 scale=rs32[:, 4 * grp + t: 4 * grp + t + 1],
             )
@@ -186,76 +184,89 @@ def tile_sign_flipped_core_sketch_h1_kernel(
         def quant_h(n):
             nc.vector.quantize_mx(out=h_cd[n][:].bitcast(FP8X4), scales=h_sc[n][:], in_=hin[n % 2][:])
 
-        def permute_rc(h):
-            words = rc[:, :, 512 * h: 512 * (h + 1)].bitcast(F32)
-            nc.scalar.copy(out=rcp[h][:], in_=words.rearrange("p b (c u) -> p b u c", u=2))
-
-        def turn_rc(h, u):
-            for b in range(PB):
-                nc.tensor.transpose(bank[4 + 2 * h + u][:, P * b: P * (b + 1)], rcp[h][:, b, u, :], ident[:])
-
-        def scale_rc(h, u, e):
-            i = 4 * h + 2 * u + e
-            src = bank[4 + 2 * h + u][:].bitcast(BF16).rearrange("p (n e) -> p e n", e=2)[:, e, :]
-            if h == 0:
-                nc.vector.tensor_scalar(out=rcc[i][:], in0=src, scalar1=cf32[:, i: i + 1], scalar2=None, op0=MULT)
-            else:
-                nc.scalar.activation(out=rcc[i][:], in_=src, func=COPY, scale=cf32[:, i: i + 1])
-
-        def bank2(h, a):
-            return bank[B2[h][a]]
-
-        def mm2(h, a, grp):
+        def mm2(i, grp):
+            h, b = divmod(i, PB)
             n = 2 * grp + h
             nc.tensor.matmul_mx(
-                out=bank2(h, a)[:],
-                lhsT=h_cd[n][:, P * a: P * (a + 1)].bitcast(FP8X4),
-                lhsT_scale=h_sc[n][:, P * a: P * (a + 1)],
-                rhs=psi[:, grp, :].bitcast(FP4X4),
-                rhs_scale=psi_sc[:, grp, :],
+                out=bank[B2[i]][:],
+                lhsT=psi[:, grp, 2 * P * b: 2 * P * (b + 1)].bitcast(FP4X4),
+                lhsT_scale=psi_sc[:, grp, P * b: P * (b + 1)],
+                rhs=h_cd[n][:].bitcast(FP8X4),
+                rhs_scale=h_sc[n][:],
                 start=(grp == 0),
                 stop=(grp == MG - 1),
             )
 
-        def finish_y(h, a, c0=0, c1=PW):
-            i = 4 * h + a
-            nc.vector.scalar_tensor_tensor(
-                out=yf[h][:, a, c0:c1], in0=bank2(h, a)[:, c0:c1], scalar=cf32[:, i: i + 1], in1=rcc[i][:, c0:c1],
-                op0=MULT, op1=ADD,
+        def unit2(i):
+            for grp in range(MG):
+                mm2(i, grp)
+
+        def shift_y(i, c0=0, c1=512):
+            h, b = divmod(i, PB)
+            nc.vector.tensor_tensor(
+                out=shifted[i % 3][:, c0:c1], in0=bank[B2[i]][:, c0:c1], in1=rc[:, b, 512 * h + c0: 512 * h + c1], op=ADD
             )
 
-        def weave_y(h, c0=0, c1=PW):
-            nc.vector.tensor_copy(
-                out=y16[h][:, 4 * c0: 4 * c1].rearrange("p (c i t) -> p c t i", i=4, t=4),
-                in_=yf[h][:, :, c0:c1].rearrange("p t (c i) -> p c t i", i=4),
+        def scale_y(i, c0=0, c1=512):
+            h = i // PB
+            eng = nc.gpsimd if i in POOL_MUL else nc.vector
+            eng.tensor_tensor(
+                out=yo[i][:, c0:c1], in0=shifted[i % 3][:, c0:c1], in1=cf[:, 512 * h + c0: 512 * h + c1], op=MULT
             )
 
-        def quant_y(h, c0=0, c1=PW):
-            nc.vector.quantize_mx(
-                out=y_cd[h][:, c0:c1].bitcast(FP8X4), scales=y_sc[h][:, c0:c1], in_=y16[h][:, 4 * c0: 4 * c1]
-            )
-
-        def store_words(h, c0=0, c1=PW):
-            nc.sync.dma_start(
-                out=out_1[h, :, c0:c1, :].rearrange("p m t -> p (m t)").bitcast(I32), in_=y_cd[h][:, c0:c1].bitcast(I32)
-            )
-
-        def store_scales(h):
-            for q in range(4):
-                nc.sync.dma_start(
-                    out=out_2[h, 4 * q: 4 * q + 4, :].bitcast(I32), in_=y_sc[h][32 * q: 32 * q + 4, :].bitcast(I32)
-                )
-
-        def turn_y(h, a, b):
-            nc.tensor.transpose(bank[BT[b]][:, P * a: P * (a + 1)], yf[h][:, a, P * b: P * (b + 1)], ident[:])
-
-        def out_y(h, b):
-            dst = yo[(PB * h + b) % 6]
+        def round_y(i, c0=0, c1=512):
             nc.scalar.copy(
-                out=dst[:].rearrange("p (c a) -> p c a", a=4),
-                in_=bank[BT[b]][:].rearrange("p (a c) -> p c a", a=4),
+                out=yw[i][:, :, c0 // 4: c1 // 4, :],
+                in_=yo[i][:, c0:c1].rearrange("p (c u e) -> p u c e", u=2, e=2),
             )
-            nc.sync.dma_start(out=out_0[P * b: P * (b + 1), 512 * h: 512 * (h + 1)], in_=dst[:])
+
+        def scale_round_y(i):
+            h = i // PB
+            nc.vector.tensor_tensor(
+                out=yw[i][:],
+                in0=shifted[i % 3][:].rearrange("p (c u e) -> p u c e", u=2, e=2),
+                in1=cf[:, 512 * h: 512 * (h + 1)].rearrange("p (c u e) -> p u c e", u=2, e=2),
+                op=MULT,
+            )
+
+        def store_y(i):
+            h, b = divmod(i, PB)
+            nc.sync.dma_start(out=out_0[P * b: P * (b + 1), 512 * h: 512 * (h + 1)], in_=yo[i][:])
+
+        def turn_y(i0, n):
+            for u in range(2):
+                for k in range(n):
+                    src = yw[i0 + k][:, u, :, :].rearrange("p c e -> p (c e)").bitcast(F32)
+                    slot = n * u + k
+                    nc.tensor.transpose(bank[B2[i0]][:, P * slot: P * (slot + 1)], src, ident[:])
+
+        def weave_y(i0, n):
+            h, b = divmod(i0, PB)
+            nc.scalar.copy(
+                out=y16[h][:, 512 * b: 512 * (b + n)].bitcast(F32).rearrange("p (r u) -> p r u", u=2),
+                in_=bank[B2[i0]][:, 0: 256 * n].rearrange("p (u r) -> p r u", u=2),
+            )
+
+        def quant_y(i0, n):
+            h, b = divmod(i0, PB)
+            cols = slice(P * b, P * (b + n))
+            nc.vector.quantize_mx(
+                out=y_cd[h][:, cols].bitcast(FP8X4), scales=y_sc[:, h, cols], in_=y16[h][:, 512 * b: 512 * (b + n)]
+            )
+
+        def store_words(i0, n):
+            h, b = divmod(i0, PB)
+            cols = slice(P * b, P * (b + n))
+            nc.sync.dma_start(
+                out=out_1[h, :, cols, :].rearrange("p m t -> p (m t)").bitcast(I32), in_=y_cd[h][:, cols].bitcast(I32)
+            )
+
+        def store_scales(queues):
+            for q in range(4):
+                queues[q % len(queues)].dma_start(
+                    out=out_2[:, 4 * q: 4 * q + 4, :].rearrange("h r n -> r h n").bitcast(I32),
+                    in_=y_sc[32 * q: 32 * q + 4, :, :].bitcast(I32),
+                )
 
         def turn_step(j, pending):
             for g in range(KG):
@@ -271,8 +282,8 @@ def tile_sign_flipped_core_sketch_h1_kernel(
 
         permute(0, 0, nc.vector.tensor_copy)
         permute(0, 1, nc.vector.tensor_copy)
-        permute(0, 2, nc.scalar.copy)
         nc.scalar.activation(out=rs32[:], in_=rs16[:].rearrange("p g t -> p (g t)"), func=COPY)
+        permute(0, 2, nc.scalar.copy)
         for g in range(KG):
             turn_x(0, g)
             sign_out(g)
@@ -290,80 +301,81 @@ def tile_sign_flipped_core_sketch_h1_kernel(
         tile1(0, 1, 0)
         tile1(0, 1, 1)
 
-        for j in range(1, PAIRS):
-            if j + 1 < PAIRS:
-                turn_step(j + 1, j - 2 if j >= 2 else None)
-            else:
-                for h in range(LH):
-                    for u in range(2):
-                        turn_rc(h, u)
-                scale_rc(0, 0, 0)
-                quant_h(j - 2)
-                scale_rc(0, 0, 1)
-                scale_rc(0, 1, 0)
-                scale_rc(0, 1, 1)
+        for j in range(1, PAIRS - 2):
+            turn_step(j + 1, j - 2 if j >= 2 else None)
             if j % 2 == 0:
                 weave_h(j - 1, nc.vector.tensor_copy)
-            if j == 5:
-                nc.scalar.activation(out=cf32[:], in_=cf16[:].rearrange("p h t -> p (h t)"), func=COPY)
-            side = []
-            if j + 2 < PAIRS:
-                side = [lambda g=g: permute(j + 2, g, nc.scalar.copy) for g in range(KG)]
-            elif j + 2 == PAIRS:
-                side = [lambda h=h: permute_rc(h) for h in range(LH)]
-            for work in side[:2]:
-                work()
+            permute(j + 2, 0, nc.scalar.copy)
+            permute(j + 2, 1, nc.scalar.copy)
             tile1(j, 0, 0)
-            for work in side[2:]:
-                work()
+            permute(j + 2, 2, nc.scalar.copy)
             tile1(j, 0, 1)
             if j % 2 == 1:
                 weave_h(j - 1, nc.vector.tensor_copy)
             tile1(j, 1, 0)
             tile1(j, 1, 1)
+        turn_step(7, None)
+        quant_h(4)
+        weave_h(5, nc.vector.tensor_copy)
+        tile1(6, 0, 0)
+        tile1(6, 0, 1)
+        tile1(6, 1, 0)
+        tile1(7, 0, 0)
+        tile1(7, 0, 1)
+        quant_h(5)
+        weave_h(6, nc.vector.tensor_copy)
+        tile1(6, 1, 1)
+        tile1(7, 1, 0)
+        tile1(7, 1, 1)
+
+        def finish(i):
+            scale_y(i)
+            round_y(i)
+            store_y(i)
+
+        def planes(i0, n):
+            turn_y(i0, n)
+            weave_y(i0, n)
 
         quant_h(6)
         weave_h(7, nc.scalar.copy)
-        for u in range(2):
-            for e in range(2):
-                scale_rc(1, u, e)
-        for a in range(2):
-            for grp in range(MG - 1):
-                mm2(0, a, grp)
-        for a in range(2):
-            mm2(0, a, MG - 1)
-            finish_y(0, a)
+        unit2(0)
+        shift_y(0)
+        finish(0)
+        unit2(1)
+        shift_y(1)
         quant_h(7)
-        for a in range(2, 4):
-            for grp in range(MG):
-                mm2(0, a, grp)
-            finish_y(0, a)
-        for a in range(4):
-            for grp in range(MG):
-                mm2(1, a, grp)
-            if a == 0:
-                weave_y(0)
-                for b in range(PB):
-                    for t in range(4):
-                        turn_y(0, t, b)
-                    out_y(0, b)
-            if a < 3:
-                finish_y(1, a)
-            if a == 0:
-                quant_y(0)
-                store_words(0)
-                store_scales(0)
-        finish_y(1, 3, 0, 256)
-        finish_y(1, 3, 256, 512)
-        for half in range(2):
-            for b in (2 * half, 2 * half + 1):
-                for t in range(3):
-                    turn_y(1, t, b)
-            for b in (2 * half, 2 * half + 1):
-                turn_y(1, 3, b)
-                out_y(1, b)
-            weave_y(1, 256 * half, 256 * (half + 1))
-        for half in range(2):
-            quant_y(1, 256 * half, 256 * (half + 1))
-            store_words(1, 256 * half, 256 * (half + 1))
-        store_scales(1)
+        finish(1)
+        unit2(2)
+        shift_y(2)
+        unit2(3)
+        shift_y(3)
+        finish(2)
+        unit2(4)
+        finish(3)
+        shift_y(4)
+        unit2(5)
+        shift_y(5)
+        finish(4)
+        unit2(6)
+        planes(0, 2)
+        planes(2, 2)
+        finish(5)
+        shift_y(6)
+        unit2(7)
+        finish(6)
+        shift_y(7)
+        quant_y(0, 4)
+        store_words(0, 4)
+        planes(4, 2)
+        planes(6, 1)
+        scale_round_y(7)
+        scale_y(7)
+        store_y(7)
+        quant_y(4, 2)
+        planes(7, 1)
+        quant_y(6, 1)
+        store_words(4, 3)
+        quant_y(7, 1)
+        store_words(7, 1)
+        store_scales([nc.scalar, nc.sync])

@@ -39,18 +39,18 @@ def tile_sign_flipped_core_sketch_h1_kernel(
         ps = ctx.enter_context(tc.psum_pool(name="ps", bufs=1))
 
         def tiles(name, count, shape, dtype):
-            return [sb.tile(shape, dtype, name="%s%d" % (name, i), align_bytes=64) for i in range(count)]
+            return [sb.tile(shape, dtype, name="%s%d" % (name, i), align_bytes=256) for i in range(count)]
 
         bank = [ps.tile([P, 512], F32, name="bank%d" % i) for i in range(8)]
-        ident = sb.tile([P, P], F32, name="ident", align_bytes=64)
-        sgn = sb.tile([P, KG, 4], BF16, name="sgn", align_bytes=64)
-        rs16 = sb.tile([P, MG, 4], BF16, name="rs16", align_bytes=64)
-        rs32 = sb.tile([P, MG * 4], F32, name="rs32", align_bytes=64)
-        cf = sb.tile([P, L], BF16, name="cf", align_bytes=64)
+        ident = sb.tile([P, P], F32, name="ident", align_bytes=256)
+        sgn = sb.tile([P, KG, 4], BF16, name="sgn", align_bytes=256)
+        rs16 = sb.tile([P, MG, 4], BF16, name="rs16", align_bytes=256)
+        rs32 = sb.tile([P, MG * 4], F32, name="rs32", align_bytes=256)
+        cf = sb.tile([P, L], BF16, name="cf", align_bytes=256)
         om = tiles("om", LH, [P, KG, 1024], U8)
         om_sc = tiles("om_sc", LH, [P, KG, 512], U8)
-        psi = sb.tile([P, MG, 2 * PW], U8, name="psi", align_bytes=64)
-        psi_sc = sb.tile([P, MG, PW], U8, name="psi_sc", align_bytes=64)
+        psi = sb.tile([P, MG, 2 * PW], U8, name="psi", align_bytes=256)
+        psi_sc = sb.tile([P, MG, PW], U8, name="psi_sc", align_bytes=256)
         xc = [tiles("xc%d_" % j, KG, [P, 2, 512], BF16) for j in range(CHUNKED)]
         xw = tiles("xw", PAIRS - CHUNKED, [P, 2, K], BF16)
         xp = [tiles("xp%d_" % i, KG, [P, 2, 2, P], F32) for i in range(2)]
@@ -61,13 +61,13 @@ def tile_sign_flipped_core_sketch_h1_kernel(
         hin = tiles("hin", 2, [P, 2048], BF16)
         h_cd = tiles("h_cd", MG * LH, [P, 512], U32)
         h_sc = tiles("h_sc", MG * LH, [P, 512], U8)
-        rc = sb.tile([P, PB, L], BF16, name="rc", align_bytes=64)
+        rc = sb.tile([P, PB, L], BF16, name="rc", align_bytes=256)
         shifted = tiles("shifted", 3, [P, 512], F32)
         yo = tiles("yo", LH * PB, [P, 512], F32)
         yw = tiles("yw", LH * PB, [P, 2, P, 2], BF16)
         y16 = tiles("y16_", LH, [P, 2048], BF16)
         y_cd = tiles("y_cd", LH, [P, PW], U32)
-        y_sc = sb.tile([P, LH, PW], U8, name="y_sc", align_bytes=64)
+        y_sc = sb.tile([P, LH, PW], U8, name="y_sc", align_bytes=256)
 
         ctx.enter_context(tc.manual_schedule())
 
@@ -101,16 +101,17 @@ def tile_sign_flipped_core_sketch_h1_kernel(
         nc.vector.memset(om_sc[1][:].rearrange("p g n -> p (g n)").bitcast(I32), 0)
         nc.vector.memset(psi_sc[:].rearrange("p g n -> p (g n)").bitcast(I32), 0)
         nc.scalar.dma_start(out=sgn[:], in_=signs.rearrange("(g c t) -> c g t", c=P, t=4))
-        nc.scalar.dma_start(out=rs16[:], in_=row_scale.rearrange("(g c t) -> c g t", c=P, t=4))
         load_x(0, 0)
-        load_scales(om_sc[0], omega_scales[:, :, 0:512])
         load_x(0, 1)
         load_x(0, 2)
         load_om(0, 0, KG)
-        for g in range(KG):
-            load_x(1, g)
-        load_scales(om_sc[1], omega_scales[:, :, 512:1024])
+        load_scales(om_sc[0], omega_scales[:, :, 0:512])
+        nc.sync.dma_start(out=rs16[:], in_=row_scale.rearrange("(g c t) -> c g t", c=P, t=4))
+        load_x(1, 0)
+        load_x(1, 1)
+        load_x(1, 2)
         load_om(1, 0, KG)
+        load_scales(om_sc[1], omega_scales[:, :, 512:1024])
         for j in range(2, PAIRS):
             if j < CHUNKED:
                 for g in range(KG):
@@ -175,14 +176,16 @@ def tile_sign_flipped_core_sketch_h1_kernel(
                 mm1(j, h, s, g)
             evac_h(j, h, s)
 
-        def weave_h(n, copy):
+        def weave_h(n, copy, c0=0, c1=512):
             copy(
-                out=hin[n % 2][:].rearrange("p (c i t) -> p c t i", i=4, t=4),
-                in_=h16[n % 4][:].rearrange("p t (c i) -> p c t i", i=4),
+                out=hin[n % 2][:, 4 * c0: 4 * c1].rearrange("p (c i t) -> p c t i", i=4, t=4),
+                in_=h16[n % 4][:, :, c0:c1].rearrange("p t (c i) -> p c t i", i=4),
             )
 
-        def quant_h(n):
-            nc.vector.quantize_mx(out=h_cd[n][:].bitcast(FP8X4), scales=h_sc[n][:], in_=hin[n % 2][:])
+        def quant_h(n, c0=0, c1=512):
+            nc.vector.quantize_mx(
+                out=h_cd[n][:, c0:c1].bitcast(FP8X4), scales=h_sc[n][:, c0:c1], in_=hin[n % 2][:, 4 * c0: 4 * c1]
+            )
 
         def mm2(i, grp):
             h, b = divmod(i, PB)
@@ -282,12 +285,16 @@ def tile_sign_flipped_core_sketch_h1_kernel(
 
         permute(0, 0, nc.vector.tensor_copy)
         permute(0, 1, nc.vector.tensor_copy)
-        nc.scalar.activation(out=rs32[:], in_=rs16[:].rearrange("p g t -> p (g t)"), func=COPY)
         permute(0, 2, nc.scalar.copy)
+        nc.scalar.activation(out=rs32[:], in_=rs16[:].rearrange("p g t -> p (g t)"), func=COPY)
         for g in range(KG):
             turn_x(0, g)
-            sign_out(g)
-            quant_a(0, g)
+        sign_out(0)
+        quant_a(0, 0)
+        sign_out(1)
+        sign_out(2)
+        quant_a(0, 1)
+        quant_a(0, 2)
         for g in range(KG):
             permute(1, g, nc.scalar.copy)
         for g in range(KG):
@@ -322,12 +329,6 @@ def tile_sign_flipped_core_sketch_h1_kernel(
         tile1(6, 1, 0)
         tile1(7, 0, 0)
         tile1(7, 0, 1)
-        quant_h(5)
-        weave_h(6, nc.vector.tensor_copy)
-        tile1(6, 1, 1)
-        tile1(7, 1, 0)
-        tile1(7, 1, 1)
-
         def finish(i):
             scale_y(i)
             round_y(i)
@@ -337,6 +338,11 @@ def tile_sign_flipped_core_sketch_h1_kernel(
             turn_y(i0, n)
             weave_y(i0, n)
 
+        quant_h(5)
+        weave_h(6, nc.vector.tensor_copy)
+        tile1(6, 1, 1)
+        tile1(7, 1, 0)
+        tile1(7, 1, 1)
         quant_h(6)
         weave_h(7, nc.scalar.copy)
         unit2(0)

from contextlib import ExitStack

import concourse.mybir as mybir
from concourse.masks import make_identity

M, K, L, PW = 2048, 1536, 1024, 512
FLOPS = 2 * M * K * L + 2 * PW * M * L

F32 = mybir.dt.float32
BF16 = mybir.dt.bfloat16
U32 = mybir.dt.uint32
I32 = mybir.dt.int32
U8 = mybir.dt.uint8
FP8X4 = mybir.dt.float8_e4m3fn_x4
FP4X4 = mybir.dt.float4_e2m1fn_x4
COPY = mybir.ActivationFunctionType.Copy
MULT = mybir.AluOpType.mult
ADD = mybir.AluOpType.add

P = 128
KG = K // 512
MG = M // 512
LH = L // 512
PAIRS = 2 * MG
PB = PW // P
CHUNKED = 3
DIRECT = ()
B2 = (4, 5, 6, 7, 0, 1, 2, 3)
POOL_MUL = ()


def tile_sign_flipped_core_sketch_h1_kernel(
    tc, x, signs, omega_words, omega_scales, row_scale, psi_words, psi_scales, running_core, coef,
    out_0, out_1, out_2,
):
    nc = tc.nc
    with ExitStack() as ctx:
        sb = ctx.enter_context(tc.tile_pool(name="sb", bufs=1))
        ps = ctx.enter_context(tc.psum_pool(name="ps", bufs=1))

        def tiles(name, count, shape, dtype):
            return [sb.tile(shape, dtype, name="%s%d" % (name, i), align_bytes=256) for i in range(count)]

        bank = [ps.tile([P, 512], F32, name="bank%d" % i) for i in range(8)]
        ident = sb.tile([P, P], F32, name="ident", align_bytes=256)
        sgn = sb.tile([P, KG, 4], BF16, name="sgn", align_bytes=256)
        rs16 = sb.tile([P, MG, 4], BF16, name="rs16", align_bytes=256)
        rs32 = sb.tile([P, MG * 4], F32, name="rs32", align_bytes=256)
        cf = sb.tile([P, L], BF16, name="cf", align_bytes=256)
        om = tiles("om", LH, [P, KG, 1024], U8)
        om_sc = tiles("om_sc", LH, [P, KG, 512], U8)
        psi = sb.tile([P, MG, 2 * PW], U8, name="psi", align_bytes=256)
        psi_sc = sb.tile([P, MG, PW], U8, name="psi_sc", align_bytes=256)
        xc = [tiles("xc%d_" % j, KG, [P, 2, 512], BF16) for j in range(CHUNKED)]
        xw = tiles("xw", PAIRS - CHUNKED, [P, 2, K], BF16)
        xp = [tiles("xp%d_" % i, KG, [P, 2, 2, P], F32) for i in range(2)]
        a16 = tiles("a16_", 3, [P, 1024], BF16)
        a_cd = [tiles("a_cd%d_" % i, KG, [P, 256], U32) for i in range(2)]
        a_sc = [tiles("a_sc%d_" % i, KG, [P, 256], U8) for i in range(2)]
        h16 = tiles("h16_", 4, [P, 4, 512], BF16)
        hin = tiles("hin", 2, [P, 2048], BF16)
        h_cd = tiles("h_cd", MG * LH, [P, 512], U32)
        h_sc = tiles("h_sc", MG * LH, [P, 512], U8)
        rc = sb.tile([P, PB, L], BF16, name="rc", align_bytes=256)
        shifted = tiles("shifted", 3, [P, 512], F32)
        yo = tiles("yo", LH * PB, [P, 512], F32)
        yw = tiles("yw", LH * PB, [P, 2, P, 2], BF16)
        y16 = tiles("y16_", LH, [P, 2048], BF16)
        y_cd = tiles("y_cd", LH, [P, PW], U32)
        y_sc = sb.tile([P, LH, PW], U8, name="y_sc", align_bytes=256)

        ctx.enter_context(tc.manual_schedule())

        def x_rows(j):
            rows = x[512 * (j // 2): 512 * (j // 2 + 1), :].rearrange("(c t) k -> c t k", t=4)
            return rows[:, 2 * (j % 2): 2 * (j % 2) + 2, :]

        def x_chunk(j, g):
            if j < CHUNKED:
                return xc[j][g][:]
            return xw[j - CHUNKED][:, :, 512 * g: 512 * (g + 1)]

        def load_scales(plane, scales):
            for q in range(4):
                nc.sync.dma_start(
                    out=plane[32 * q: 32 * q + 4, :, :].bitcast(I32),
                    in_=scales[:, 4 * q: 4 * q + 4, :].rearrange("g r n -> r g n").bitcast(I32),
                )

        def load_om(h, g0, g1):
            nc.sync.dma_start(
                out=om[h][:, g0:g1, :].bitcast(I32),
                in_=omega_words[g0:g1, :, 1024 * h: 1024 * (h + 1)].rearrange("g p b -> p g b").bitcast(I32),
            )

        def load_x(j, g):
            nc.sync.dma_start(out=x_chunk(j, g), in_=x_rows(j)[:, :, 512 * g: 512 * (g + 1)])

        make_identity(nc, ident[:])
        nc.vector.memset(om_sc[0][:].rearrange("p g n -> p (g n)").bitcast(I32), 0)
        nc.vector.memset(om_sc[1][:].rearrange("p g n -> p (g n)").bitcast(I32), 0)
        nc.vector.memset(psi_sc[:].rearrange("p g n -> p (g n)").bitcast(I32), 0)
        nc.scalar.dma_start(out=sgn[:], in_=signs.rearrange("(g c t) -> c g t", c=P, t=4))
        load_x(0, 0)
        load_x(0, 1)
        load_x(0, 2)
        load_om(0, 0, KG)
        load_scales(om_sc[0], omega_scales[:, :, 0:512])
        nc.sync.dma_start(out=rs16[:], in_=row_scale.rearrange("(g c t) -> c g t", c=P, t=4))
        load_x(1, 0)
        load_x(1, 1)
        load_x(1, 2)
        load_om(1, 0, KG)
        load_scales(om_sc[1], omega_scales[:, :, 512:1024])
        for j in range(2, PAIRS):
            if j < CHUNKED:
                for g in range(KG):
                    load_x(j, g)
            else:
                nc.sync.dma_start(out=xw[j - CHUNKED][:], in_=x_rows(j))
        nc.sync.dma_start(out=rc[:], in_=running_core.rearrange("(b p) l -> p b l", p=P))
        load_scales(psi_sc, psi_scales)
        nc.sync.dma_start(out=psi[:].bitcast(I32), in_=psi_words.rearrange("g p b -> p g b").bitcast(I32))
        nc.sync.dma_start(out=cf[:], in_=coef.partition_broadcast(P))


        def permute(j, g, copy):
            if j in DIRECT:
                return
            words = x_chunk(j, g).bitcast(F32)
            copy(out=xp[j % 2][g][:], in_=words.rearrange("p s (c u) -> p s u c", u=2))

        def turn_x(j, g):
            for u in range(2):
                for s in range(2):
                    if j in DIRECT:
                        src = x_chunk(j, g)[:, s, :].bitcast(F32)[:, u:256:2]
                    else:
                        src = xp[j % 2][g][:, s, u, :]
                    slot = 2 * u + s
                    nc.tensor.transpose(bank[4 + g][:, P * slot: P * (slot + 1)], src, ident[:])

        def sign_out(g):
            nc.vector.tensor_tensor(
                out=a16[g][:].rearrange("p (r u e) -> p r u e", u=2, e=2),
                in0=bank[4 + g][:].bitcast(BF16).rearrange("p (u r e) -> p r u e", u=2, e=2),
                in1=sgn[:, g, :].rearrange("p (u e) -> p u e", u=2).unsqueeze(1).to_broadcast([P, 256, 2, 2]),
                op=MULT,
            )

        def quant_a(j, g):
            nc.vector.quantize_mx(out=a_cd[j % 2][g][:].bitcast(FP8X4), scales=a_sc[j % 2][g][:], in_=a16[g][:])

        def mm1(j, h, s, g):
            nc.tensor.matmul_mx(
                out=bank[2 * h + s][:],
                lhsT=a_cd[j % 2][g][:, P * s: P * (s + 1)].bitcast(FP8X4),
                lhsT_scale=a_sc[j % 2][g][:, P * s: P * (s + 1)],
                rhs=om[h][:, g, :].bitcast(FP4X4),
                rhs_scale=om_sc[h][:, g, :],
                start=(g == 0),
                stop=(g == KG - 1),
            )

        def evac_h(j, h, s):
            grp, t = j // 2, 2 * (j % 2) + s
            nc.scalar.activation(
                out=h16[(2 * grp + h) % 4][:, t, :],
                in_=bank[2 * h + s][:],
                func=COPY,
                scale=rs32[:, 4 * grp + t: 4 * grp + t + 1],
            )

        def tile1(j, h, s):
            for g in range(KG):
                mm1(j, h, s, g)
            evac_h(j, h, s)

        def weave_h(n, copy, c0=0, c1=512):
            copy(
                out=hin[n % 2][:, 4 * c0: 4 * c1].rearrange("p (c i t) -> p c t i", i=4, t=4),
                in_=h16[n % 4][:, :, c0:c1].rearrange("p t (c i) -> p c t i", i=4),
            )

        def quant_h(n, c0=0, c1=512):
            nc.vector.quantize_mx(
                out=h_cd[n][:, c0:c1].bitcast(FP8X4), scales=h_sc[n][:, c0:c1], in_=hin[n % 2][:, 4 * c0: 4 * c1]
            )

        def mm2(i, grp):
            h, b = divmod(i, PB)
            n = 2 * grp + h
            nc.tensor.matmul_mx(
                out=bank[B2[i]][:],
                lhsT=psi[:, grp, 2 * P * b: 2 * P * (b + 1)].bitcast(FP4X4),
                lhsT_scale=psi_sc[:, grp, P * b: P * (b + 1)],
                rhs=h_cd[n][:].bitcast(FP8X4),
                rhs_scale=h_sc[n][:],
                start=(grp == 0),
                stop=(grp == MG - 1),
            )

        def unit2(i):
            for grp in range(MG):
                mm2(i, grp)

        def shift_y(i, c0=0, c1=512):
            h, b = divmod(i, PB)
            nc.vector.tensor_tensor(
                out=shifted[i % 3][:, c0:c1], in0=bank[B2[i]][:, c0:c1], in1=rc[:, b, 512 * h + c0: 512 * h + c1], op=ADD
            )

        def scale_y(i, c0=0, c1=512):
            h = i // PB
            eng = nc.gpsimd if i in POOL_MUL else nc.vector
            eng.tensor_tensor(
                out=yo[i][:, c0:c1], in0=shifted[i % 3][:, c0:c1], in1=cf[:, 512 * h + c0: 512 * h + c1], op=MULT
            )

        def round_y(i, c0=0, c1=512):
            nc.scalar.copy(
                out=yw[i][:, :, c0 // 4: c1 // 4, :],
                in_=yo[i][:, c0:c1].rearrange("p (c u e) -> p u c e", u=2, e=2),
            )

        def scale_round_y(i):
            h = i // PB
            nc.vector.tensor_tensor(
                out=yw[i][:],
                in0=shifted[i % 3][:].rearrange("p (c u e) -> p u c e", u=2, e=2),
                in1=cf[:, 512 * h: 512 * (h + 1)].rearrange("p (c u e) -> p u c e", u=2, e=2),
                op=MULT,
            )

        def store_y(i):
            h, b = divmod(i, PB)
            nc.sync.dma_start(out=out_0[P * b: P * (b + 1), 512 * h: 512 * (h + 1)], in_=yo[i][:])

        def turn_y(i0, n):
            for u in range(2):
                for k in range(n):
                    src = yw[i0 + k][:, u, :, :].rearrange("p c e -> p (c e)").bitcast(F32)
                    slot = n * u + k
                    nc.tensor.transpose(bank[B2[i0]][:, P * slot: P * (slot + 1)], src, ident[:])

        def weave_y(i0, n):
            h, b = divmod(i0, PB)
            nc.scalar.copy(
                out=y16[h][:, 512 * b: 512 * (b + n)].bitcast(F32).rearrange("p (r u) -> p r u", u=2),
                in_=bank[B2[i0]][:, 0: 256 * n].rearrange("p (u r) -> p r u", u=2),
            )

        def quant_y(i0, n):
            h, b = divmod(i0, PB)
            cols = slice(P * b, P * (b + n))
            nc.vector.quantize_mx(
                out=y_cd[h][:, cols].bitcast(FP8X4), scales=y_sc[:, h, cols], in_=y16[h][:, 512 * b: 512 * (b + n)]
            )

        def store_words(i0, n):
            h, b = divmod(i0, PB)
            cols = slice(P * b, P * (b + n))
            nc.sync.dma_start(
                out=out_1[h, :, cols, :].rearrange("p m t -> p (m t)").bitcast(I32), in_=y_cd[h][:, cols].bitcast(I32)
            )

        def store_scales(queues):
            for q in range(4):
                queues[q % len(queues)].dma_start(
                    out=out_2[:, 4 * q: 4 * q + 4, :].rearrange("h r n -> r h n").bitcast(I32),
                    in_=y_sc[32 * q: 32 * q + 4, :, :].bitcast(I32),
                )

        def turn_step(j, pending):
            for g in range(KG):
                turn_x(j, g)
            sign_out(0)
            if pending is not None:
                quant_h(pending)
            sign_out(1)
            quant_a(j, 0)
            sign_out(2)
            quant_a(j, 1)
            quant_a(j, 2)

        permute(0, 0, nc.vector.tensor_copy)
        permute(0, 1, nc.vector.tensor_copy)
        permute(0, 2, nc.scalar.copy)
        nc.scalar.activation(out=rs32[:], in_=rs16[:].rearrange("p g t -> p (g t)"), func=COPY)
        for g in range(KG):
            turn_x(0, g)
        sign_out(0)
        quant_a(0, 0)
        sign_out(1)
        sign_out(2)
        quant_a(0, 1)
        quant_a(0, 2)
        for g in range(KG):
            permute(1, g, nc.scalar.copy)
        for g in range(KG):
            for s in range(2):
                mm1(0, 0, s, g)
        for s in range(2):
            evac_h(0, 0, s)
        turn_step(1, None)
        for g in range(KG):
            permute(2, g, nc.scalar.copy)
        tile1(0, 1, 0)
        tile1(0, 1, 1)

        for j in range(1, PAIRS - 2):
            turn_step(j + 1, j - 2 if j >= 2 else None)
            if j % 2 == 0:
                weave_h(j - 1, nc.vector.tensor_copy)
            permute(j + 2, 0, nc.scalar.copy)
            permute(j + 2, 1, nc.scalar.copy)
            tile1(j, 0, 0)
            permute(j + 2, 2, nc.scalar.copy)
            tile1(j, 0, 1)
            if j % 2 == 1:
                weave_h(j - 1, nc.vector.tensor_copy)
            tile1(j, 1, 0)
            tile1(j, 1, 1)
        turn_step(7, None)
        quant_h(4)
        weave_h(5, nc.vector.tensor_copy)
        tile1(6, 0, 0)
        tile1(6, 0, 1)
        tile1(6, 1, 0)
        tile1(7, 0, 0)
        tile1(7, 0, 1)
        def finish(i):
            scale_y(i)
            round_y(i)
            store_y(i)

        def planes(i0, n):
            turn_y(i0, n)
            weave_y(i0, n)

        quant_h(5)
        weave_h(6, nc.vector.tensor_copy)
        tile1(6, 1, 1)
        tile1(7, 1, 0)
        tile1(7, 1, 1)
        quant_h(6)
        weave_h(7, nc.scalar.copy)
        unit2(0)
        shift_y(0)
        finish(0)
        unit2(1)
        shift_y(1)
        quant_h(7)
        finish(1)
        unit2(2)
        shift_y(2)
        unit2(3)
        shift_y(3)
        finish(2)
        unit2(4)
        finish(3)
        shift_y(4)
        unit2(5)
        shift_y(5)
        finish(4)
        unit2(6)
        planes(0, 2)
        planes(2, 2)
        finish(5)
        shift_y(6)
        unit2(7)
        finish(6)
        shift_y(7)
        quant_y(0, 4)
        store_words(0, 4)
        planes(4, 2)
        planes(6, 1)
        scale_round_y(7)
        scale_y(7)
        store_y(7)
        quant_y(4, 2)
        planes(7, 1)
        quant_y(6, 1)
        store_words(4, 3)
        quant_y(7, 1)
        store_words(7, 1)
        store_scales([nc.scalar, nc.sync])
